import numpy as np
import ml_dtypes


def mxq(x, axis, fmt="e4m3"):
    dtype, down = {"e4m3": (ml_dtypes.float8_e4m3fn, 7), "e5m2": (ml_dtypes.float8_e5m2, 14)}[fmt]
    v = np.moveaxis(np.asarray(x, np.float32).astype(ml_dtypes.bfloat16).astype(np.float64), axis, -1)
    blocks = v.reshape(v.shape[:-1] + (-1, 32))
    amax = np.abs(blocks).max(-1, keepdims=True)
    byte = np.maximum(np.where(amax > 0, np.frexp(amax)[1] - 1 + 127, 0) - down, 1)
    scale = np.exp2(byte - 127.0)
    codes = (blocks / scale).astype(np.float32).astype(dtype).astype(np.float64)
    return np.moveaxis((codes * scale).reshape(v.shape), -1, axis)


WIDE = False


def mx_kscale(k):
    if not WIDE:
        return np.ones(k)
    levels = np.array([10, -10, 5, -5, 0])
    if k % 512:
        return np.exp2(np.random.permutation(np.resize(levels, k // 32))).repeat(32)
    a = np.empty((k // 512, 16))
    for p in range(k // 512):
        a[p, :8] = np.random.permutation(np.resize(levels, 8))
        for g in range(8):
            far = levels[np.abs(levels - a[p, g]) >= 10]
            a[p, g + 8] = far[np.random.randint(len(far))]
    return np.exp2(a.ravel()).repeat(32)


BF16 = ml_dtypes.bfloat16


def bf(x):
    return np.asarray(x, np.float32).astype(BF16)


def f64(x):
    return np.asarray(x).astype(np.float64)


E2M1 = np.array([0.0, 0.5, 1.0, 1.5, 2.0, 3.0, 4.0, 6.0, -0.0, -0.5, -1.0, -1.5, -2.0, -3.0, -4.0, -6.0])


def pack_weight(w, fmt):
    k, n = w.shape
    w = f64(bf(w)).reshape(k // 32, 32, n)
    amax = np.abs(w).max(1)
    if fmt == "e4m3":
        byte = np.frexp(amax)[1] - 1 + 127 - 7
    else:
        mant, ex = np.frexp(amax / 6.0)
        byte = np.where(mant > 0.5, ex, ex - 1) + 127
    byte = np.clip(np.where(amax > 0, byte, 1), 1, 254)
    scaled = (w * np.exp2(127.0 - byte)[:, None, :]).reshape(k, n).astype(np.float32)
    by_word = np.ascontiguousarray(scaled.reshape(k // 512, 128, 4, n).transpose(0, 1, 3, 2))
    if fmt == "e4m3":
        words = by_word.astype(ml_dtypes.float8_e4m3fn).view(np.uint8)
    else:
        c = by_word.astype(ml_dtypes.float4_e2m1fn).view(np.uint8) & 0xF
        words = c[..., 0::2] | (c[..., 1::2] << 4)
    return np.ascontiguousarray(words), np.ascontiguousarray(byte.astype(np.uint8).reshape(k // 512, 16, n))


def unpack_weight(words, scales, fmt):
    g, p, n, _ = words.shape
    if fmt == "e4m3":
        vals = np.ascontiguousarray(words).view(ml_dtypes.float8_e4m3fn).astype(np.float64)
    else:
        nib = np.empty((g, p, n, 4), np.uint8)
        nib[..., 0::2] = words & 0xF
        nib[..., 1::2] = words >> 4
        vals = E2M1[nib]
    vals = vals * np.repeat(np.exp2(scales.astype(np.float64) - 127.0), 8, axis=1)[..., None]
    return vals.transpose(0, 1, 3, 2).reshape(g * 512, n)
def pack4(w):
    words, scales = pack_weight(w, "e2m1")
    return words.reshape(words.shape[0], 128, -1), scales


def unpack4(words, scales):
    return unpack_weight(words.reshape(words.shape[0], 128, -1, 2), scales, "e2m1")


S, N, C, R = 1536, 1024, 512, 512

SHOCK = 0.7
SPREAD = 0.2


def draw0():
    s = mx_kscale(N)
    t = mx_kscale(N)
    u = mx_kscale(S)
    shocks = SHOCK * np.random.standard_normal((S, N))
    inverse = np.random.standard_normal((N, N)) ** 2 / np.sqrt(3 * N)
    baskets = np.random.standard_normal((N, C)) / np.sqrt(N)
    words, scales = pack4(baskets / t[:, None])
    contrasts = np.random.standard_normal((R, S)) / np.sqrt(S)
    return {"shocks": bf(shocks * s),
            "inverse": bf(inverse / s[:, None]),
            "base": bf((1 + SPREAD * np.random.standard_normal(N)) * t),
            "weight": bf((1 + SPREAD * np.random.standard_normal(S)) * u),
            "basket_words": words, "basket_scales": scales,
            "contrasts": bf(contrasts / u)}


def core(shocks, inverse, base, weight, basket_words, basket_scales, contrasts):
    moves = mxq(f64(shocks), 1, "e4m3") @ mxq(f64(inverse), 0, "e4m3")
    rel = np.exp(moves)
    priced = mxq(rel * f64(base)[None, :], 1, "e4m3")
    index = priced @ unpack4(basket_words, basket_scales)
    weighted = mxq(rel * f64(weight)[:, None], 0, "e4m3")
    contrast = mxq(f64(contrasts), 1, "e4m3") @ weighted
    return index, contrast


def e4m3fn_bytes(y):
    return np.clip(np.asarray(y, np.float64), -448.0, 448.0).astype(np.float32).astype(ml_dtypes.float8_e4m3fn).view(np.uint8)


def e4m3fn_values(b):
    return np.asarray(b, np.uint8).view(ml_dtypes.float8_e4m3fn).astype(np.float64)


def setup_inputs():
    d = draw0()
    x0 = np.asarray(d['shocks']).astype(np.float64)
    s = (np.max(np.abs(x0), axis=(0,), keepdims=True) / 448.0).astype(np.float32)
    out = {}
    for k, v in d.items():
        if k == 'shocks':
            out['shocks_bytes'] = e4m3fn_bytes(x0 / s.astype(np.float64))
            out['shocks_scale'] = s
        else:
            out[k] = v
    return out


def reference(shocks_bytes, shocks_scale, inverse, base, weight, basket_words, basket_scales, contrasts):
    return core(e4m3fn_values(shocks_bytes) * shocks_scale.astype(np.float64), inverse, base, weight, basket_words, basket_scales, contrasts)

from contextlib import ExitStack

import concourse.mybir as mybir
from concourse.masks import make_identity

S, N, C, R = 1536, 1024, 512, 512
FLOPS = 2 * (S * N * N + S * N * C + R * S * N)

F32 = mybir.dt.float32
BF16 = mybir.dt.bfloat16
I32 = mybir.dt.int32
U32 = mybir.dt.uint32
U8 = mybir.dt.uint8
FP8 = mybir.dt.float8_e4m3fn
FP8X4 = mybir.dt.float8_e4m3fn_x4
FP4X4 = mybir.dt.float4_e2m1fn_x4
MULT = mybir.AluOpType.mult
EXP = mybir.ActivationFunctionType.Exp

P = 128
T = 4
KP = P * T
SG = S // KP
KQ = N // KP
NJ = N // KP

BLOCKS = ((0, 0), (0, 1), (1, 0), (2, 0), (2, 1), (1, 1))


def tile_ghosh_price_push_s8_kernel(
    tc, shocks_bytes, shocks_scale, inverse, base, weight, basket_words, basket_scales, contrasts, out_0, out_1
):
    nc = tc.nc
    with ExitStack() as ctx:
        keep = ctx.enter_context(tc.tile_pool(name="keep", bufs=1))
        work = ctx.enter_context(tc.tile_pool(name="work", bufs=3))
        psum = ctx.enter_context(tc.psum_pool(name="psum", bufs=2))

        sh_bytes = keep.tile([P, SG * T, N], U8, name="sh_bytes", align_bytes=64)
        scale_kp = keep.tile([P, KQ, T], F32, name="scale_kp")
        scale_row = keep.tile([P, N], F32, name="scale_row")
        inv_raw = keep.tile([P, NJ, KQ, T, KP], BF16, name="inv_raw")
        base_kp = keep.tile([P, NJ, T], BF16, name="base_kp")
        weight_kp = keep.tile([P, SG, T], BF16, name="weight_kp")
        weight_f32 = keep.tile([P, SG, T], F32, name="weight_f32")
        b_words = keep.tile([P, NJ, 2 * C], U8, name="b_words", align_bytes=64)
        b_scales = keep.tile([P, NJ, C], U8, name="b_scales", align_bytes=64)
        con_raw = keep.tile([P, T, S], BF16, name="con_raw")

        sh_codes = keep.tile([P, SG * T, KQ, P], U32, name="sh_codes", align_bytes=64)
        sh_scales = keep.tile([P, SG * T, KQ, P], U8, name="sh_scales", align_bytes=64)
        inv_codes = keep.tile([P, NJ, KQ, KP], U32, name="inv_codes", align_bytes=64)
        inv_scales = keep.tile([P, NJ, KQ, KP], U8, name="inv_scales", align_bytes=64)
        con_codes = keep.tile([P, SG, R], U32, name="con_codes", align_bytes=64)
        con_scales = keep.tile([P, SG, R], U8, name="con_scales", align_bytes=64)
        pr_codes = keep.tile([P, SG, NJ, KP], U32, name="pr_codes", align_bytes=64)
        pr_scales = keep.tile([P, SG, NJ, KP], U8, name="pr_scales", align_bytes=64)
        we_codes = keep.tile([P, SG, NJ, KP], U32, name="we_codes", align_bytes=64)
        we_scales = keep.tile([P, SG, NJ, KP], U8, name="we_scales", align_bytes=64)

        ident = keep.tile([P, P], F32, name="ident")
        warm = keep.tile([P, 1], F32, name="warm")

        nc.vector.memset(warm[:], 0.0)
        nc.vector.memset(b_scales[:].rearrange("p j n -> p (j n)").bitcast(I32), 0)
        nc.scalar.activation(out=warm[:], in_=warm[:], func=EXP)
        make_identity(nc, ident[:])

        shocks_v = shocks_bytes.rearrange("(g m t) k -> g m t k", m=P, t=T)

        def load_shocks(g, t0, t1):
            nc.sync.dma_start(out=sh_bytes[:, T * g + t0 : T * g + t1, :], in_=shocks_v[g][:, t0:t1, :])

        inverse_v = inverse.rearrange("(q p t) n -> q p t n", p=P, t=T)

        def load_inverse(j, q):
            nc.sync.dma_start(out=inv_raw[:, j, q], in_=inverse_v[q][:, :, KP * j : KP * (j + 1)])

        nc.sync.dma_start(out=scale_kp[:], in_=shocks_scale.rearrange("o (q p t) -> p (o q) t", p=P, t=T))
        load_shocks(0, 0, 2)
        load_inverse(0, 0)
        load_inverse(0, 1)
        load_shocks(0, 2, 4)
        nc.sync.dma_start(out=scale_row[:], in_=shocks_scale.rearrange("o k -> (o k)").partition_broadcast(P))
        load_inverse(1, 0)
        load_inverse(1, 1)
        nc.sync.dma_start(out=base_kp[:], in_=base.rearrange("(j p t) -> p j t", p=P, t=T))
        nc.sync.dma_start(out=weight_kp[:], in_=weight.rearrange("(g p t) -> p g t", p=P, t=T))
        load_shocks(1, 0, 4)
        load_shocks(2, 0, 4)
        con_v = contrasts.rearrange("(a r) k -> r a k", r=P)
        nc.sync.dma_start(out=con_raw[:, 0:2], in_=con_v[:, 0:2])
        nc.sync.dma_start(out=con_raw[:, 2:4], in_=con_v[:, 2:4])
        for quad in range(4):
            nc.sync.dma_start(
                out=b_scales[32 * quad : 32 * quad + 4].bitcast(I32),
                in_=basket_scales.rearrange("j s n -> s j n")[4 * quad : 4 * quad + 4].bitcast(I32),
            )
        nc.sync.dma_start(out=b_words[:], in_=basket_words.rearrange("j p b -> p j b"))

        sh_wide = {}
        sh_bank = {}
        sh_group = {}

        def widen_plain(i, engine):
            x = work.tile([P, N], BF16, name="xb", bufs=4)
            sh_wide[i] = x
            if engine == "scalar":
                nc.scalar.copy(out=x[:], in_=sh_bytes[:, i, :].bitcast(FP8))
            else:
                nc.vector.tensor_copy(out=x[:], in_=sh_bytes[:, i, :].bitcast(FP8))

        def widen_scaled(i):
            x = work.tile([P, N], BF16, name="xb", bufs=4)
            sh_wide[i] = x
            nc.vector.tensor_tensor(out=x[:], in0=sh_bytes[:, i, :].bitcast(FP8), in1=scale_row[:], op=MULT)

        def turn_shocks(i):
            bank = psum.tile([P, KQ, 2, P], F32, name="tr", bufs=3)
            sh_bank[i] = bank
            words = sh_wide[i][:].bitcast(F32)
            for q in range(KQ):
                for u in range(2):
                    nc.tensor.transpose(bank[:, q, u, :], words[:, 256 * q + u : 256 * (q + 1) : 2], ident[:])

        def group_tile(i):
            if i % 2 == 0:
                sh_group[i // 2] = work.tile([P, 2, KQ * P * T], BF16, name="xg", bufs=2, align_bytes=64)
            return sh_group[i // 2][:, i % 2, :]

        def empty_shocks_scaled(i):
            g = group_tile(i).rearrange("p (q r u e) -> p q r u e", q=KQ, u=2, e=2)
            b = sh_bank[i][:].rearrange("p q u r -> p (q u r)").bitcast(BF16)
            b = b.rearrange("p (q u r e) -> p q r u e", q=KQ, u=2, e=2)
            for q in range(KQ):
                sc = scale_kp[:, q, :].rearrange("p (u e) -> p u e", u=2).unsqueeze(1).to_broadcast([P, P, 2, 2])
                nc.vector.tensor_tensor(out=g[:, q], in0=b[:, q], in1=sc, op=MULT)

        def empty_shocks(i):
            g = group_tile(i).bitcast(F32).rearrange("p (q r u) -> p q r u", q=KQ, u=2)
            nc.scalar.copy(out=g, in_=sh_bank[i][:].rearrange("p q u r -> p q r u"))

        def quantize_shocks(k):
            nc.vector.quantize_mx(
                out=sh_codes[:, 2 * k : 2 * k + 2].rearrange("p i q r -> p (i q r)").bitcast(FP8X4),
                scales=sh_scales[:, 2 * k : 2 * k + 2].rearrange("p i q r -> p (i q r)"),
                in_=sh_group[k][:].rearrange("p i c -> p (i c)"),
            )

        inv_group = {}

        def group_inverse(j, q, engine, c0, c1):
            if (j, q) not in inv_group:
                inv_group[j, q] = work.tile([P, KP, T], BF16, name="ig", bufs=2, align_bytes=64)
            dst = inv_group[j, q][:, c0:c1, :].rearrange("p (c i) t -> p c t i", i=4)
            src = inv_raw[:, j, q, :, c0:c1].rearrange("p t (c i) -> p c t i", i=4)
            if engine == "scalar":
                nc.scalar.copy(out=dst, in_=src)
            else:
                nc.vector.tensor_copy(out=dst, in_=src)

        def quantize_inverse(j, q):
            nc.vector.quantize_mx(
                out=inv_codes[:, j, q, :].bitcast(FP8X4),
                scales=inv_scales[:, j, q, :],
                in_=inv_group[j, q][:].rearrange("p n t -> p (n t)"),
            )

        con_bank = {}
        con_group = {}

        def turn_contrasts(g, a0):
            bank = psum.tile([P, 2, 2, P], F32, name="tr", bufs=3)
            con_bank[g, a0] = bank
            for a in range(2):
                words = con_raw[:, a0 + a, :].bitcast(F32)
                for u in range(2):
                    nc.tensor.transpose(bank[:, a, u, :], words[:, 256 * g + u : 256 * (g + 1) : 2], ident[:])

        def empty_contrasts(g, a0):
            if a0 == 0:
                con_group[g] = work.tile([P, R * T], BF16, name="cg", bufs=2, align_bytes=64)
            dst = con_group[g][:].bitcast(F32).rearrange("p (a r u) -> p a r u", r=P, u=2)[:, a0 : a0 + 2]
            nc.scalar.copy(out=dst, in_=con_bank[g, a0][:].rearrange("p a u r -> p a r u"))

        def quantize_contrasts(g):
            nc.vector.quantize_mx(out=con_codes[:, g, :].bitcast(FP8X4), scales=con_scales[:, g, :], in_=con_group[g][:])

        mv_bank = {}
        rel = {}
        tr_bank = {}
        priced = {}
        weighted = {}

        def unit(h, i):
            return h // 2, BLOCKS[h // 2][0], BLOCKS[h // 2][1], 2 * (h % 2) + i

        def moves(h):
            for i in range(2):
                b, g, j, t = unit(h, i)
                bank = psum.tile([P, KP], F32, name="mm", bufs=3)
                mv_bank[h, i] = bank
                for q in range(KQ):
                    nc.tensor.matmul_mx(
                        out=bank[:],
                        lhsT=sh_codes[:, T * g + t, q, :].bitcast(FP8X4),
                        lhsT_scale=sh_scales[:, T * g + t, q, :],
                        rhs=inv_codes[:, j, q, :].bitcast(FP8X4),
                        rhs_scale=inv_scales[:, j, q, :],
                        start=(q == 0),
                        stop=(q == KQ - 1),
                    )

        def relatives(h):
            for i in range(2):
                b, g, j, t = unit(h, i)
                if t == 0:
                    rel[b] = work.tile([P, T, KP], F32, name="rel", bufs=3)
                nc.scalar.activation(
                    out=rel[b][:, t, :].rearrange("p (v m) -> p v m", v=T),
                    in_=mv_bank[h, i][:].rearrange("p (m v) -> p v m", v=T),
                    func=EXP,
                )

        def turn(h):
            for i in range(2):
                b, g, j, t = unit(h, i)
                bank = psum.tile([P, T, P], F32, name="tr", bufs=3)
                tr_bank[h, i] = bank
                for v in range(T):
                    nc.tensor.transpose(bank[:, v, :], rel[b][:, t, P * v : P * (v + 1)], ident[:])

        def price(h):
            priced[h] = work.tile([P, 2, P, T], BF16, name="pr", bufs=3, align_bytes=64)
            for i in range(2):
                b, g, j, t = unit(h, i)
                nc.vector.tensor_tensor(
                    out=priced[h][:, i],
                    in0=tr_bank[h, i][:].rearrange("p v m -> p m v"),
                    in1=base_kp[:, j, :].unsqueeze(1).to_broadcast([P, P, T]),
                    op=MULT,
                )

        def quantize_priced(h):
            b, g, j, t = unit(h, 0)
            cols = slice(P * t, P * (t + 2))
            nc.vector.quantize_mx(
                out=pr_codes[:, g, j, cols].bitcast(FP8X4),
                scales=pr_scales[:, g, j, cols],
                in_=priced[h][:].rearrange("p i m v -> p (i m v)"),
            )

        def weigh(b, half):
            g = BLOCKS[b][0]
            weighted[b, half] = work.tile([P, KP // 2, T], BF16, name="we", bufs=3, align_bytes=64)
            cols = slice(KP // 2 * half, KP // 2 * (half + 1))
            nc.vector.tensor_tensor(
                out=weighted[b, half][:],
                in0=rel[b][:, :, cols].rearrange("p t n -> p n t"),
                in1=weight_kp[:, g, :].unsqueeze(1).to_broadcast([P, KP // 2, T]),
                op=MULT,
            )

        scaled = {}

        def scale_units(h):
            for i in range(2):
                b, g, j, t = unit(h, i)
                if t == 0:
                    scaled[b] = work.tile([P, T, KP], BF16, name="sc", bufs=2)
                nc.scalar.activation(
                    out=scaled[b][:, t, :],
                    in_=rel[b][:, t, :],
                    func=mybir.ActivationFunctionType.Copy,
                    scale=weight_f32[:, g, t : t + 1],
                )

        def interleave(b, half):
            weighted[b, half] = work.tile([P, KP // 2, T], BF16, name="we", bufs=3, align_bytes=64)
            cols = slice(KP // 2 * half, KP // 2 * (half + 1))
            nc.vector.tensor_copy(
                out=weighted[b, half][:].rearrange("p (c i) t -> p c t i", i=4),
                in_=scaled[b][:, :, cols].rearrange("p t (c i) -> p c t i", i=4),
            )

        def quantize_weighted(b, half):
            g, j = BLOCKS[b]
            cols = slice(KP // 2 * half, KP // 2 * (half + 1))
            nc.vector.quantize_mx(
                out=we_codes[:, g, j, cols].bitcast(FP8X4),
                scales=we_scales[:, g, j, cols],
                in_=weighted[b, half][:].rearrange("p n t -> p (n t)"),
            )

        index_v = out_0.rearrange("(g m t) c -> g m t c", m=P, t=T)
        acc_bank = {}

        def index_mm(g, t):
            bank = psum.tile([P, C], F32, name="acc", bufs=2)
            acc_bank[0, g, t] = bank
            for j in range(NJ):
                nc.tensor.matmul_mx(
                    out=bank[:],
                    lhsT=pr_codes[:, g, j, P * t : P * (t + 1)].bitcast(FP8X4),
                    lhsT_scale=pr_scales[:, g, j, P * t : P * (t + 1)],
                    rhs=b_words[:, j, :].bitcast(FP4X4),
                    rhs_scale=b_scales[:, j, :],
                    start=(j == 0),
                    stop=(j == NJ - 1),
                )

        def index_out(g, t, engine):
            res = work.tile([P, C], F32, name="res", bufs=8)
            if engine == "scalar":
                nc.scalar.copy(out=res[:], in_=acc_bank[0, g, t][:])
            else:
                nc.vector.tensor_copy(out=res[:], in_=acc_bank[0, g, t][:])
            nc.sync.dma_start(out=index_v[g][:, t, :], in_=res[:])

        def contrast_mm(a, j, name, bufs):
            bank = psum.tile([P, KP], F32, name=name, bufs=bufs)
            acc_bank[1, a, j] = bank
            for n, g in enumerate((0, 2, 1)):
                nc.tensor.matmul_mx(
                    out=bank[:],
                    lhsT=con_codes[:, g, P * a : P * (a + 1)].bitcast(FP8X4),
                    lhsT_scale=con_scales[:, g, P * a : P * (a + 1)],
                    rhs=we_codes[:, g, j, :].bitcast(FP8X4),
                    rhs_scale=we_scales[:, g, j, :],
                    start=(n == 0),
                    stop=(n == SG - 1),
                )

        def contrast_out(a, j, engine):
            res = work.tile([P, KP], F32, name="res", bufs=8)
            dst = res[:].rearrange("p (m v) -> p m v", v=T)
            src = acc_bank[1, a, j][:].rearrange("p (v m) -> p m v", v=T)
            if engine == "scalar":
                nc.scalar.copy(out=dst, in_=src)
            else:
                nc.vector.tensor_copy(out=dst, in_=src)
            nc.sync.dma_start(out=out_1[P * a : P * (a + 1), KP * j : KP * (j + 1)], in_=res[:])

        widen_plain(0, "vector")
        widen_plain(1, "scalar")
        turn_shocks(0)
        group_inverse(0, 0, "scalar", 0, KP)
        turn_shocks(1)
        empty_shocks_scaled(0)
        empty_shocks_scaled(1)
        group_inverse(0, 1, "scalar", 0, 3 * KP // 4)
        group_inverse(0, 1, "vector", 3 * KP // 4, KP)
        quantize_shocks(0)
        quantize_inverse(0, 0)
        widen_plain(2, "scalar")
        turn_shocks(2)
        widen_plain(3, "scalar")
        quantize_inverse(0, 1)
        moves(0)
        turn_shocks(3)
        empty_shocks_scaled(2)
        empty_shocks_scaled(3)
        relatives(0)
        nc.vector.tensor_copy(out=weight_f32[:], in_=weight_kp[:])
        widen_scaled(4)
        quantize_shocks(1)

        for h in range(12):
            if h > 0:
                moves(h)
                relatives(h)
            if h == 0:
                group_inverse(1, 0, "scalar", 0, KP)
                group_inverse(1, 1, "scalar", 0, KP)
                widen_scaled(5)
                widen_scaled(6)
                quantize_inverse(1, 0)
            if h == 1:
                turn_shocks(4)
                turn_shocks(5)
                empty_shocks(4)
                empty_shocks(5)
                widen_scaled(7)
                quantize_inverse(1, 1)
                quantize_shocks(2)
            if h == 2:
                turn_shocks(6)
                turn_shocks(7)
                empty_shocks(6)
                empty_shocks(7)
                widen_scaled(8)
                widen_scaled(9)
                quantize_shocks(3)
            if h == 3:
                turn_shocks(8)
                turn_shocks(9)
                empty_shocks(8)
                empty_shocks(9)
                widen_scaled(10)
                widen_scaled(11)
                quantize_shocks(4)
            if h == 4:
                turn_shocks(10)
                turn_shocks(11)
                empty_shocks(10)
                empty_shocks(11)
            if h in (2, 3):
                weigh(0, h % 2)
            if h >= 3:
                scale_units(h - 1)
            if h >= 4 and h % 2 == 1:
                interleave(h // 2 - 1, 0)
                interleave(h // 2 - 1, 1)
            if h == 4:
                quantize_shocks(5)
            if h in (5, 6, 7):
                turn_contrasts(h - 5, 0)
                turn_contrasts(h - 5, 2)
                empty_contrasts(h - 5, 0)
                empty_contrasts(h - 5, 2)
            if h >= 1:
                turn(h - 1)
                price(h - 1)
            if h in (2, 3):
                quantize_weighted(0, h % 2)
            if h >= 4 and h % 2 == 1:
                quantize_weighted(h // 2 - 1, 0)
                quantize_weighted(h // 2 - 1, 1)
            if h in (5, 6, 7):
                quantize_contrasts(h - 5)
            if h >= 1:
                quantize_priced(h - 1)
            if h in (5, 6):
                for t in (0, 1):
                    index_mm(0, 2 * (h - 5) + t)
                for t in (0, 1):
                    index_out(0, 2 * (h - 5) + t, "scalar")
            if h in (10, 11):
                for a in (0, 1):
                    contrast_mm(2 * (h - 10) + a, 0, "acc", 2)
                for a in (0, 1):
                    contrast_out(2 * (h - 10) + a, 0, "scalar")

        turn(11)
        scale_units(11)
        index_mm(2, 0)
        index_mm(2, 1)
        index_out(2, 0, "scalar")
        index_out(2, 1, "scalar")
        price(11)
        interleave(5, 0)
        interleave(5, 1)
        quantize_priced(11)
        quantize_weighted(5, 0)
        quantize_weighted(5, 1)
        index_mm(2, 2)
        index_mm(2, 3)
        index_out(2, 2, "scalar")
        index_out(2, 3, "vector")
        index_mm(1, 0)
        index_mm(1, 1)
        index_out(1, 0, "scalar")
        index_out(1, 1, "vector")
        for a in range(3):
            contrast_mm(a, 1, "mm", 3)
        index_mm(1, 2)
        index_mm(1, 3)
        index_out(1, 2, "scalar")
        contrast_out(0, 1, "vector")
        contrast_out(1, 1, "scalar")
        contrast_out(2, 1, "vector")
        contrast_mm(3, 1, "tr", 3)
        index_out(1, 3, "scalar")
        contrast_out(3, 1, "vector")
